import numpy as np
import ml_dtypes


def mxq(x, axis, fmt="e4m3"):
    dtype, down = {"e4m3": (ml_dtypes.float8_e4m3fn, 7), "e5m2": (ml_dtypes.float8_e5m2, 14)}[fmt]
    v = np.moveaxis(np.asarray(x, np.float32).astype(ml_dtypes.bfloat16).astype(np.float64), axis, -1)
    blocks = v.reshape(v.shape[:-1] + (-1, 32))
    amax = np.abs(blocks).max(-1, keepdims=True)
    byte = np.maximum(np.where(amax > 0, np.frexp(amax)[1] - 1 + 127, 0) - down, 1)
    scale = np.exp2(byte - 127.0)
    codes = (blocks / scale).astype(np.float32).astype(dtype).astype(np.float64)
    return np.moveaxis((codes * scale).reshape(v.shape), -1, axis)


WIDE = False


def mx_kscale(k):
    if not WIDE:
        return np.ones(k)
    levels = np.array([10, -10, 5, -5, 0])
    if k % 512:
        return np.exp2(np.random.permutation(np.resize(levels, k // 32))).repeat(32)
    a = np.empty((k // 512, 16))
    for p in range(k // 512):
        a[p, :8] = np.random.permutation(np.resize(levels, 8))
        for g in range(8):
            far = levels[np.abs(levels - a[p, g]) >= 10]
            a[p, g + 8] = far[np.random.randint(len(far))]
    return np.exp2(a.ravel()).repeat(32)


def f64(x):
    return np.asarray(x).astype(np.float64)


def striped(idx):
    return np.tile(idx.reshape(-1, 16).T, (8, 1)).astype(np.uint16)


def unstriped(offs):
    return offs[:16].T.reshape(-1).astype(np.int64)


def pack_weight(w):
    k, n = w.shape
    w = f64(np.asarray(w, np.float32).astype(ml_dtypes.bfloat16)).reshape(k // 32, 32, n)
    amax = np.abs(w).max(1)
    byte = np.clip(np.where(amax > 0, np.frexp(amax)[1] - 1 + 127 - 7, 1), 1, 254)
    scaled = (w * np.exp2(127.0 - byte)[:, None, :]).reshape(k, n).astype(np.float32)
    words = np.ascontiguousarray(scaled.reshape(k // 512, 128, 4, n).transpose(0, 1, 3, 2)).astype(ml_dtypes.float8_e4m3fn).view(np.uint8)
    return words, np.ascontiguousarray(byte.astype(np.uint8).reshape(k // 512, 16, n))


def unpack_weight(words, scales):
    g, p, n, _ = words.shape
    vals = np.ascontiguousarray(words).view(ml_dtypes.float8_e4m3fn).astype(np.float64) * np.repeat(np.exp2(scales.astype(np.float64) - 127.0), 8, axis=1)[..., None]
    return vals.transpose(0, 1, 3, 2).reshape(g * 512, n)


K, T, S, D, N = 512, 4096, 1024, 4, 256
P = 2 ** 7


def setup_inputs():
    n = np.random.standard_normal
    s = mx_kscale(K)[:, None]
    packed_xT = pack_weight(n((K, T)) * s)
    return {
        "x_words": packed_xT[0],
        "x_scales": packed_xT[1],
        "w1": (n((K, N)) / np.sqrt(K) / s).astype(np.float32),
        "w2": (n((K, N)) / np.sqrt(K) / s).astype(np.float32),
        "ago": (np.tile(np.random.uniform(0.1, 2.5, S), (P, 1))).astype(np.float32),
        "amt": (np.tile(np.random.uniform(0.5, 2.0, S), (P, 1))).astype(np.float32),
        "ec50": (np.random.uniform(0.3, 1.5, (N, 1))).astype(np.float32),
        "offs": striped(np.random.permutation(T)[:S]),
    }


def reference(x_words, x_scales, w1, w2, ago, amt, ec50, offs):
    xq = unpack_weight(x_words, x_scales)[:, unstriped(offs)]
    ya = mxq(f64(w1), 0, "e4m3").T @ xq
    fast = np.log(np.exp(ya) + 1.0) + 0.4
    ef = np.exp(-1.0 * (fast * f64(ago)[:1]))
    yb = mxq(f64(w2), 0, "e4m3").T @ xq
    slow = 0.4 * (np.log(np.exp(yb) + 1.0))
    es = np.exp(-1.0 * (slow * f64(ago)[:1]))
    cd = f64(amt)[:1] * (0.7 * ef + 0.3 * es)
    conc = cd.reshape(len(cd), -1, D).sum(axis=2)
    return conc / (conc + f64(ec50))

@@ -1,0 +1,170 @@
+import math
+from contextlib import ExitStack
+
+import concourse.mybir as mybir
+from concourse.masks import make_identity
+
+K, T, S, D, N = 512, 4096, 1024, 4, 256
+P = 128
+PACK = 4
+GROUPS = S // (P * D)
+M_BLOCKS = N // P
+FLOPS = 2 * 2 * K * S * N
+
+F32 = mybir.dt.float32
+BF16 = mybir.dt.bfloat16
+I32 = mybir.dt.int32
+U32 = mybir.dt.uint32
+U16 = mybir.dt.uint16
+U8 = mybir.dt.uint8
+FP8X4 = mybir.dt.float8_e4m3fn_x4
+ALU = mybir.AluOpType
+ACT = mybir.ActivationFunctionType
+
+LN_CAP = 2.0 ** 60
+
+
+def tile_picked_ypkpd_eff_p_kernel(
+    tc, x_words, x_scales, w1, w2, ago, amt, ec50, offs, out
+):
+    nc = tc.nc
+    with ExitStack() as ctx:
+        sb = ctx.enter_context(tc.tile_pool(name="sb", bufs=1))
+        ps = ctx.enter_context(tc.psum_pool(name="ps", bufs=1))
+
+        offsets = sb.tile([P, S // 16], U16, name="offsets")
+        nc.sync.dma_start(offsets[:], offs)
+
+        table_scales = sb.tile([P, T], U8, name="table_scales")
+        nc.vector.memset(table_scales[:].bitcast(I32), 0)
+
+        w_raw = [sb.tile([P, PACK, N], F32, name=f"w_raw{c}") for c in range(2)]
+        table_words = sb.tile([P, T], I32, name="table_words")
+        nc.sync.dma_start(w_raw[0][:], w1.rearrange("(p t) m -> p t m", t=PACK))
+        for r in range(4):
+            nc.sync.dma_start(table_scales[r:P:32, :].bitcast(I32), x_scales[0, r:16:4, :].bitcast(I32))
+        nc.sync.dma_start(table_words[:], x_words[0].rearrange("p n t -> p (n t)").bitcast(I32))
+        nc.sync.dma_start(w_raw[1][:], w2.rearrange("(p t) m -> p t m", t=PACK))
+
+        ago_t = sb.tile([P, GROUPS, D], F32, name="ago_t")
+        amt_t = sb.tile([P, GROUPS, D], F32, name="amt_t")
+        ec_t = sb.tile([P, M_BLOCKS], F32, name="ec_t")
+        nc.sync.dma_start(ago_t[:], ago[0].rearrange("(g p d) -> p g d", g=GROUPS, d=D))
+        nc.sync.dma_start(amt_t[:], amt[0].rearrange("(g p d) -> p g d", g=GROUPS, d=D))
+        with nc.allow_non_contiguous_dma(reason="one value a partition"):
+            nc.sync.dma_start(ec_t[:], ec50.rearrange("(b p) o -> p (b o)", p=P))
+
+        ident = sb.tile([P, P], F32, name="ident")
+        make_identity(nc, ident[:])
+
+        w_codes = [sb.tile([P, N], U32, name=f"w_codes{c}", align_bytes=64) for c in range(2)]
+        w_scales = [sb.tile([P, N], U8, name=f"w_scales{c}", align_bytes=64) for c in range(2)]
+        w_bf = [sb.tile([P, N, PACK], BF16, name=f"w_bf{c}", align_bytes=64) for c in range(2)]
+
+        def round_weights(c):
+            nc.vector.tensor_copy(
+                w_bf[c][:].rearrange("p (a i) t -> p a t i", i=4),
+                w_raw[c][:].rearrange("p t (a i) -> p a t i", i=4),
+            )
+
+        def quantise_weights(c):
+            nc.vector.quantize_mx(
+                out=w_codes[c][:].bitcast(FP8X4), scales=w_scales[c][:], in_=w_bf[c][:].rearrange("p m t -> p (m t)")
+            )
+
+        picked_scales = sb.tile([P, S], U8, name="picked_scales")
+        x_sc = sb.tile([P, GROUPS, D, P], U8, name="x_sc", align_bytes=64)
+        x_codes = [sb.tile([P, D, P], U32, name=f"x_codes{g}", align_bytes=64) for g in range(GROUPS)]
+
+        round_weights(0)
+        nc.vector.tensor_copy(picked_scales[:], table_scales[:].indirect(offsets[:]))
+        quantise_weights(0)
+        nc.vector.tensor_copy(x_sc[:], picked_scales[:].rearrange("p (g v d) -> p g d v", g=GROUPS, d=D))
+
+        cols = P * D // 16
+        for g in range(GROUPS):
+            nc.vector.tensor_copy(
+                x_codes[g][:].rearrange("p d v -> p v d"),
+                table_words[:].bitcast(U32).indirect(offsets[:, g * cols : (g + 1) * cols]),
+            )
+        round_weights(1)
+        quantise_weights(1)
+
+        neg_ago = sb.tile([P, GROUPS, D], F32, name="neg_ago")
+        slow_scale = sb.tile([P, GROUPS, D], F32, name="slow_scale")
+        fast_bias = sb.tile([P, GROUPS, D], F32, name="fast_bias")
+        weight = sb.tile([P, GROUPS, D], F32, name="weight")
+        nc.gpsimd.tensor_scalar(neg_ago[:], ago_t[:], -1.0, 0.0, ALU.mult, ALU.add)
+        nc.gpsimd.tensor_scalar(slow_scale[:], ago_t[:], -0.4, 0.0, ALU.mult, ALU.add)
+        nc.gpsimd.tensor_scalar(fast_bias[:], ago_t[:], -0.4, math.log(0.7 / 0.3), ALU.mult, ALU.add)
+        nc.gpsimd.tensor_scalar(weight[:], amt_t[:], 0.3, 0.0, ALU.mult, ALU.add)
+
+        banks = [(c, g, h) for c in range(2) for g in range(GROUPS) for h in range(D // 2)]
+        NB = len(banks)
+        y = {}
+        ey = sb.tile([P, NB, 2, N], F32, name="ey")
+        u = sb.tile([P, NB, 2, N], F32, name="u")
+        for b, (c, g, h) in enumerate(banks):
+            y[b] = ps.tile([P, 2, N], F32, name=f"y{b}", tag=f"bank{b}")
+            for e in range(2):
+                d = 2 * h + e
+                nc.tensor.matmul_mx(
+                    out=y[b][:, e, :],
+                    lhsT=x_codes[g][:, d, :].bitcast(FP8X4),
+                    lhsT_scale=x_sc[:, g, d, :],
+                    rhs=w_codes[c][:].bitcast(FP8X4),
+                    rhs_scale=w_scales[c][:],
+                    start=True,
+                    stop=True,
+                )
+            nc.scalar.activation(ey[:, b], y[b][:], ACT.Exp)
+            nc.vector.tensor_scalar(u[:, b], ey[:, b], LN_CAP, 1.0, ALU.min, ALU.add)
+
+        lnu = sb.tile([P, 2, NB // 2, 2 * N], F32, name="lnu")
+        sp = sb.tile([P, NB, 2, N], F32, name="sp")
+        u_pairs = u[:].rearrange("p (c b) e m -> p c b (e m)", c=2)
+        order = []
+        for pair in range(NB // 2):
+            nc.scalar.activation(lnu[:, :, pair, :], u_pairs[:, :, pair, :], ACT.Ln)
+            for c in range(2):
+                b = c * (NB // 2) + pair
+                order.append(b)
+                nc.vector.tensor_tensor(
+                    sp[:, b].rearrange("p e m -> p (e m)"), y[b][:].rearrange("p e m -> p (e m)"), lnu[:, c, pair, :], ALU.max
+                )
+
+        q = 0
+        for mb in range(M_BLOCKS):
+            for g in range(GROUPS):
+                conc = ps.tile([P, P], F32, name=f"conc{q}", tag=f"bank{order[q]}")
+                for d in range(D):
+                    decay = sb.tile([P, 2, P], F32, name=f"decay{q}_{d}")
+                    dose = sb.tile([P, 2, P], F32, name=f"dose{q}_{d}")
+                    fast = banks.index((0, g, d // 2))
+                    slow = banks.index((1, g, d // 2))
+                    nc.scalar.activation(
+                        decay[:, 0, :], sp[:, fast, d % 2, mb * P : (mb + 1) * P], ACT.Exp,
+                        bias=fast_bias[:, g, d : d + 1], scale=neg_ago[:, g, d : d + 1],
+                    )
+                    nc.scalar.activation(
+                        decay[:, 1, :], sp[:, slow, d % 2, mb * P : (mb + 1) * P], ACT.Exp, scale=slow_scale[:, g, d : d + 1]
+                    )
+                    scaler = nc.vector if q == 0 else nc.gpsimd
+                    scaler.tensor_scalar(dose[:], decay[:], weight[:, g, d : d + 1], 0.0, ALU.mult, ALU.add)
+                    for c in range(2):
+                        nc.tensor.matmul(
+                            conc[:], dose[:, c, :], ident[:], is_transpose=True,
+                            start=(d == 0 and c == 0), stop=(d == D - 1 and c == 1),
+                        )
+                den = sb.tile([P, P], F32, name=f"den{q}")
+                inv = sb.tile([P, P], F32, name=f"inv{q}")
+                res = sb.tile([P, P], F32, name=f"res{q}")
+                halves = [slice(0, P // 2), slice(P // 2, P)]
+                for s in halves:
+                    nc.vector.tensor_scalar(den[:, s], conc[:, s], ec_t[:, mb : mb + 1], None, ALU.add)
+                for s in halves:
+                    nc.vector.reciprocal(inv[:, s], den[:, s])
+                for s in halves:
+                    nc.vector.tensor_tensor(res[:, s], conc[:, s], inv[:, s], ALU.mult)
+                nc.sync.dma_start(out[mb * P : (mb + 1) * P, g * P : (g + 1) * P], res[:])
+                q = q + 1

@@ -90,15 +90,6 @@ def tile_picked_ypkpd_eff_p_kernel(
         round_weights(1)
         quantise_weights(1)
 
-        neg_ago = sb.tile([P, GROUPS, D], F32, name="neg_ago")
-        slow_scale = sb.tile([P, GROUPS, D], F32, name="slow_scale")
-        fast_bias = sb.tile([P, GROUPS, D], F32, name="fast_bias")
-        weight = sb.tile([P, GROUPS, D], F32, name="weight")
-        nc.gpsimd.tensor_scalar(neg_ago[:], ago_t[:], -1.0, 0.0, ALU.mult, ALU.add)
-        nc.gpsimd.tensor_scalar(slow_scale[:], ago_t[:], -0.4, 0.0, ALU.mult, ALU.add)
-        nc.gpsimd.tensor_scalar(fast_bias[:], ago_t[:], -0.4, math.log(0.7 / 0.3), ALU.mult, ALU.add)
-        nc.gpsimd.tensor_scalar(weight[:], amt_t[:], 0.3, 0.0, ALU.mult, ALU.add)
-
         banks = [(c, g, h) for c in range(2) for g in range(GROUPS) for h in range(D // 2)]
         NB = len(banks)
         y = {}
@@ -120,6 +111,15 @@ def tile_picked_ypkpd_eff_p_kernel(
             nc.scalar.activation(ey[:, b], y[b][:], ACT.Exp)
             nc.vector.tensor_scalar(u[:, b], ey[:, b], LN_CAP, 1.0, ALU.min, ALU.add)
 
+        neg_ago = sb.tile([P, GROUPS, D], F32, name="neg_ago")
+        slow_scale = sb.tile([P, GROUPS, D], F32, name="slow_scale")
+        fast_bias = sb.tile([P, GROUPS, D], F32, name="fast_bias")
+        weight = sb.tile([P, GROUPS, D], F32, name="weight")
+        nc.vector.tensor_scalar(neg_ago[:], ago_t[:], -1.0, 0.0, ALU.mult, ALU.add)
+        nc.vector.tensor_scalar(slow_scale[:], ago_t[:], -0.4, 0.0, ALU.mult, ALU.add)
+        nc.vector.tensor_scalar(fast_bias[:], ago_t[:], -0.4, math.log(0.7 / 0.3), ALU.mult, ALU.add)
+        nc.vector.tensor_scalar(weight[:], amt_t[:], 0.3, 0.0, ALU.mult, ALU.add)
+
         lnu = sb.tile([P, 2, NB // 2, 2 * N], F32, name="lnu")
         sp = sb.tile([P, NB, 2, N], F32, name="sp")
         u_pairs = u[:].rearrange("p (c b) e m -> p c b (e m)", c=2)
@@ -133,38 +133,46 @@ def tile_picked_ypkpd_eff_p_kernel(
                     sp[:, b].rearrange("p e m -> p (e m)"), y[b][:].rearrange("p e m -> p (e m)"), lnu[:, c, pair, :], ALU.max
                 )
 
-        q = 0
-        for mb in range(M_BLOCKS):
-            for g in range(GROUPS):
-                conc = ps.tile([P, P], F32, name=f"conc{q}", tag=f"bank{order[q]}")
-                for d in range(D):
-                    decay = sb.tile([P, 2, P], F32, name=f"decay{q}_{d}")
-                    dose = sb.tile([P, 2, P], F32, name=f"dose{q}_{d}")
-                    fast = banks.index((0, g, d // 2))
-                    slow = banks.index((1, g, d // 2))
-                    nc.scalar.activation(
-                        decay[:, 0, :], sp[:, fast, d % 2, mb * P : (mb + 1) * P], ACT.Exp,
-                        bias=fast_bias[:, g, d : d + 1], scale=neg_ago[:, g, d : d + 1],
+        quarters = [(mb, g) for mb in range(M_BLOCKS) for g in range(GROUPS)]
+        conc = {}
+        den = {}
+
+        def accumulate(q):
+            mb, g = quarters[q]
+            m_cols = slice(mb * P, (mb + 1) * P)
+            conc[q] = ps.tile([P, P], F32, name=f"conc{q}", tag=f"bank{order[q]}")
+            for d in range(D):
+                decay = sb.tile([P, 2, P], F32, name=f"decay{q}_{d}")
+                dose = sb.tile([P, 2, P], F32, name=f"dose{q}_{d}")
+                fast = banks.index((0, g, d // 2))
+                slow = banks.index((1, g, d // 2))
+                nc.scalar.activation(
+                    decay[:, 0, :], sp[:, fast, d % 2, m_cols], ACT.Exp,
+                    bias=fast_bias[:, g, d : d + 1], scale=neg_ago[:, g, d : d + 1],
+                )
+                nc.scalar.activation(decay[:, 1, :], sp[:, slow, d % 2, m_cols], ACT.Exp, scale=slow_scale[:, g, d : d + 1])
+                nc.vector.tensor_scalar(dose[:], decay[:], weight[:, g, d : d + 1], None, ALU.mult)
+                for c in range(2):
+                    nc.tensor.matmul(
+                        conc[q][:], dose[:, c, :], ident[:], is_transpose=True,
+                        start=(d == 0 and c == 0), stop=(d == D - 1 and c == 1),
                     )
-                    nc.scalar.activation(
-                        decay[:, 1, :], sp[:, slow, d % 2, mb * P : (mb + 1) * P], ACT.Exp, scale=slow_scale[:, g, d : d + 1]
-                    )
-                    scaler = nc.vector if q == 0 else nc.gpsimd
-                    scaler.tensor_scalar(dose[:], decay[:], weight[:, g, d : d + 1], 0.0, ALU.mult, ALU.add)
-                    for c in range(2):
-                        nc.tensor.matmul(
-                            conc[:], dose[:, c, :], ident[:], is_transpose=True,
-                            start=(d == 0 and c == 0), stop=(d == D - 1 and c == 1),
-                        )
-                den = sb.tile([P, P], F32, name=f"den{q}")
-                inv = sb.tile([P, P], F32, name=f"inv{q}")
-                res = sb.tile([P, P], F32, name=f"res{q}")
-                halves = [slice(0, P // 2), slice(P // 2, P)]
-                for s in halves:
-                    nc.vector.tensor_scalar(den[:, s], conc[:, s], ec_t[:, mb : mb + 1], None, ALU.add)
-                for s in halves:
-                    nc.vector.reciprocal(inv[:, s], den[:, s])
-                for s in halves:
-                    nc.vector.tensor_tensor(res[:, s], conc[:, s], inv[:, s], ALU.mult)
-                nc.sync.dma_start(out[mb * P : (mb + 1) * P, g * P : (g + 1) * P], res[:])
-                q = q + 1
+            den[q] = sb.tile([P, P], F32, name=f"den{q}")
+            nc.scalar.activation(den[q][:], conc[q][:], ACT.Identity, bias=ec_t[:, mb : mb + 1])
+
+        def saturate(q):
+            mb, g = quarters[q]
+            inv = sb.tile([P, P], F32, name=f"inv{q}")
+            res = sb.tile([P, P], F32, name=f"res{q}")
+            halves = [slice(0, P // 2), slice(P // 2, P)]
+            for s in halves:
+                nc.vector.reciprocal(inv[:, s], den[q][:, s])
+            for s in halves:
+                nc.vector.tensor_tensor(res[:, s], conc[q][:, s], inv[:, s], ALU.mult)
+            nc.sync.dma_start(out[mb * P : (mb + 1) * P, g * P : (g + 1) * P], res[:])
+
+        for q in range(len(quarters)):
+            accumulate(q)
+            if q > 0:
+                saturate(q - 1)
+        saturate(len(quarters) - 1)

@@ -38,21 +38,12 @@ def tile_picked_ypkpd_eff_p_kernel(
         table_scales = sb.tile([P, T], U8, name="table_scales")
         nc.vector.memset(table_scales[:].bitcast(I32), 0)
 
-        w_raw = [sb.tile([P, PACK, N], F32, name=f"w_raw{c}") for c in range(2)]
+        w_raw = [sb.tile([P, PACK, N], F32, name=f"w_raw{c}", tag=f"w_raw{c}") for c in range(2)]
         table_words = sb.tile([P, T], I32, name="table_words")
         nc.sync.dma_start(w_raw[0][:], w1.rearrange("(p t) m -> p t m", t=PACK))
-        for r in range(4):
-            nc.sync.dma_start(table_scales[r:P:32, :].bitcast(I32), x_scales[0, r:16:4, :].bitcast(I32))
+        nc.sync.dma_start(table_scales[0:P:8, :].bitcast(I32), x_scales[0].bitcast(I32))
         nc.sync.dma_start(table_words[:], x_words[0].rearrange("p n t -> p (n t)").bitcast(I32))
         nc.sync.dma_start(w_raw[1][:], w2.rearrange("(p t) m -> p t m", t=PACK))
-
-        ago_t = sb.tile([P, GROUPS, D], F32, name="ago_t")
-        amt_t = sb.tile([P, GROUPS, D], F32, name="amt_t")
-        ec_t = sb.tile([P, M_BLOCKS], F32, name="ec_t")
-        nc.sync.dma_start(ago_t[:], ago[0].rearrange("(g p d) -> p g d", g=GROUPS, d=D))
-        nc.sync.dma_start(amt_t[:], amt[0].rearrange("(g p d) -> p g d", g=GROUPS, d=D))
-        with nc.allow_non_contiguous_dma(reason="one value a partition"):
-            nc.sync.dma_start(ec_t[:], ec50.rearrange("(b p) o -> p (b o)", p=P))
 
         ident = sb.tile([P, P], F32, name="ident")
         make_identity(nc, ident[:])
@@ -62,10 +53,12 @@ def tile_picked_ypkpd_eff_p_kernel(
         w_bf = [sb.tile([P, N, PACK], BF16, name=f"w_bf{c}", align_bytes=64) for c in range(2)]
 
         def round_weights(c):
-            nc.vector.tensor_copy(
-                w_bf[c][:].rearrange("p (a i) t -> p a t i", i=4),
-                w_raw[c][:].rearrange("p t (a i) -> p a t i", i=4),
-            )
+            dst = w_bf[c][:].rearrange("p (a i) t -> p a t i", i=4)
+            src = w_raw[c][:].rearrange("p t (a i) -> p a t i", i=4)
+            if c == 0:
+                nc.scalar.activation(dst, src, ACT.Copy)
+            else:
+                nc.vector.tensor_copy(dst, src)
 
         def quantise_weights(c):
             nc.vector.quantize_mx(
@@ -73,13 +66,21 @@ def tile_picked_ypkpd_eff_p_kernel(
             )
 
         picked_scales = sb.tile([P, S], U8, name="picked_scales")
-        x_sc = sb.tile([P, GROUPS, D, P], U8, name="x_sc", align_bytes=64)
+        dealt_scales = sb.tile([P, S], U8, name="dealt_scales")
+        x_plane = sb.tile([P, S], U8, name="x_plane", align_bytes=64)
+        nc.vector.memset(x_plane[:].bitcast(I32), 0)
+        x_sc = x_plane[:].rearrange("p (g d v) -> p g d v", g=GROUPS, d=D)
         x_codes = [sb.tile([P, D, P], U32, name=f"x_codes{g}", align_bytes=64) for g in range(GROUPS)]
 
         round_weights(0)
         nc.vector.tensor_copy(picked_scales[:], table_scales[:].indirect(offsets[:]))
         quantise_weights(0)
-        nc.vector.tensor_copy(x_sc[:], picked_scales[:].rearrange("p (g v d) -> p g d v", g=GROUPS, d=D))
+        nc.vector.tensor_copy(
+            dealt_scales[:].rearrange("p (g d v) -> p g d v", g=GROUPS, d=D),
+            picked_scales[:].rearrange("p (g v d) -> p g d v", g=GROUPS, d=D),
+        )
+        for r in range(4):
+            nc.scalar.dma_start(x_plane[r:P:32, :].bitcast(I32), dealt_scales[8 * r : P : 32, :].bitcast(I32))
 
         cols = P * D // 16
         for g in range(GROUPS):
@@ -89,6 +90,15 @@ def tile_picked_ypkpd_eff_p_kernel(
             )
         round_weights(1)
         quantise_weights(1)
+
+        small = sb.tile([P, 3, GROUPS * D], F32, name="small", tag="w_raw1")
+        ago_t = small[:, 0, :].rearrange("p (g d) -> p g d", d=D)
+        amt_t = small[:, 1, :].rearrange("p (g d) -> p g d", d=D)
+        ec_t = small[:, 2, :]
+        nc.sync.dma_start(ago_t, ago[0].rearrange("(g p d) -> p g d", g=GROUPS, d=D))
+        nc.sync.dma_start(amt_t, amt[0].rearrange("(g p d) -> p g d", g=GROUPS, d=D))
+        with nc.allow_non_contiguous_dma(reason="one value a partition"):
+            nc.sync.dma_start(ec_t[:, 0:M_BLOCKS], ec50.rearrange("(b p) o -> p (b o)", p=P))
 
         banks = [(c, g, h) for c in range(2) for g in range(GROUPS) for h in range(D // 2)]
         NB = len(banks)
@@ -115,10 +125,10 @@ def tile_picked_ypkpd_eff_p_kernel(
         slow_scale = sb.tile([P, GROUPS, D], F32, name="slow_scale")
         fast_bias = sb.tile([P, GROUPS, D], F32, name="fast_bias")
         weight = sb.tile([P, GROUPS, D], F32, name="weight")
-        nc.vector.tensor_scalar(neg_ago[:], ago_t[:], -1.0, 0.0, ALU.mult, ALU.add)
-        nc.vector.tensor_scalar(slow_scale[:], ago_t[:], -0.4, 0.0, ALU.mult, ALU.add)
-        nc.vector.tensor_scalar(fast_bias[:], ago_t[:], -0.4, math.log(0.7 / 0.3), ALU.mult, ALU.add)
-        nc.vector.tensor_scalar(weight[:], amt_t[:], 0.3, 0.0, ALU.mult, ALU.add)
+        nc.vector.tensor_scalar(neg_ago[:], ago_t, -1.0, 0.0, ALU.mult, ALU.add)
+        nc.vector.tensor_scalar(slow_scale[:], ago_t, -0.4, 0.0, ALU.mult, ALU.add)
+        nc.vector.tensor_scalar(fast_bias[:], ago_t, -0.4, math.log(0.7 / 0.3), ALU.mult, ALU.add)
+        nc.vector.tensor_scalar(weight[:], amt_t, 0.3, 0.0, ALU.mult, ALU.add)
 
         lnu = sb.tile([P, 2, NB // 2, 2 * N], F32, name="lnu")
         sp = sb.tile([P, NB, 2, N], F32, name="sp")

@@ -9,7 +9,13 @@ P = 128
 PACK = 4
 GROUPS = S // (P * D)
 M_BLOCKS = N // P
-FLOPS = 2 * 2 * K * S * N
+RATES = 2
+LIST_COLS = P * D // 16
+ROW_STEP = 8
+RUN = 4
+FLOPS = 2 * RATES * K * S * N
+
+EXP_CAP = 2.0**60
 
 F32 = mybir.dt.float32
 BF16 = mybir.dt.bfloat16
@@ -20,8 +26,6 @@ U8 = mybir.dt.uint8
 FP8X4 = mybir.dt.float8_e4m3fn_x4
 ALU = mybir.AluOpType
 ACT = mybir.ActivationFunctionType
-
-LN_CAP = 2.0 ** 60
 
 
 def tile_picked_ypkpd_eff_p_kernel(
@@ -38,57 +42,45 @@ def tile_picked_ypkpd_eff_p_kernel(
         table_scales = sb.tile([P, T], U8, name="table_scales")
         nc.vector.memset(table_scales[:].bitcast(I32), 0)
 
-        w_raw = [sb.tile([P, PACK, N], F32, name=f"w_raw{c}", tag=f"w_raw{c}") for c in range(2)]
+        w_raw = [sb.tile([P, PACK, N], F32, name=f"w_raw{c}", tag=f"w_raw{c}") for c in range(RATES)]
         table_words = sb.tile([P, T], I32, name="table_words")
         nc.sync.dma_start(w_raw[0][:], w1.rearrange("(p t) m -> p t m", t=PACK))
-        nc.sync.dma_start(table_scales[0:P:8, :].bitcast(I32), x_scales[0].bitcast(I32))
+        nc.sync.dma_start(table_scales[0:P:ROW_STEP, :].bitcast(I32), x_scales[0].bitcast(I32))
         nc.sync.dma_start(table_words[:], x_words[0].rearrange("p n t -> p (n t)").bitcast(I32))
         nc.sync.dma_start(w_raw[1][:], w2.rearrange("(p t) m -> p t m", t=PACK))
 
         ident = sb.tile([P, P], F32, name="ident")
         make_identity(nc, ident[:])
 
-        w_codes = [sb.tile([P, N], U32, name=f"w_codes{c}", align_bytes=64) for c in range(2)]
-        w_scales = [sb.tile([P, N], U8, name=f"w_scales{c}", align_bytes=64) for c in range(2)]
-        w_bf = [sb.tile([P, N, PACK], BF16, name=f"w_bf{c}", align_bytes=64) for c in range(2)]
-
-        def round_weights(c):
-            dst = w_bf[c][:].rearrange("p (a i) t -> p a t i", i=4)
-            src = w_raw[c][:].rearrange("p t (a i) -> p a t i", i=4)
-            if c == 0:
-                nc.scalar.activation(dst, src, ACT.Copy)
-            else:
-                nc.vector.tensor_copy(dst, src)
+        w_codes = [sb.tile([P, N], U32, name=f"w_codes{c}", align_bytes=64) for c in range(RATES)]
+        w_scales = [sb.tile([P, N], U8, name=f"w_scales{c}", align_bytes=64) for c in range(RATES)]
+        w_bf = [sb.tile([P, N, PACK], BF16, name=f"w_bf{c}", align_bytes=64) for c in range(RATES)]
+        interleaved = [w_bf[c][:].rearrange("p (a i) t -> p a t i", i=RUN) for c in range(RATES)]
+        by_row = [w_raw[c][:].rearrange("p t (a i) -> p a t i", i=RUN) for c in range(RATES)]
 
         def quantise_weights(c):
             nc.vector.quantize_mx(
                 out=w_codes[c][:].bitcast(FP8X4), scales=w_scales[c][:], in_=w_bf[c][:].rearrange("p m t -> p (m t)")
             )
 
-        picked_scales = sb.tile([P, S], U8, name="picked_scales")
-        dealt_scales = sb.tile([P, S], U8, name="dealt_scales")
-        x_plane = sb.tile([P, S], U8, name="x_plane", align_bytes=64)
-        nc.vector.memset(x_plane[:].bitcast(I32), 0)
-        x_sc = x_plane[:].rearrange("p (g d v) -> p g d v", g=GROUPS, d=D)
-        x_codes = [sb.tile([P, D, P], U32, name=f"x_codes{g}", align_bytes=64) for g in range(GROUPS)]
+        nc.scalar.activation(interleaved[0], by_row[0], ACT.Copy)
 
-        round_weights(0)
+        picked_scales = sb.tile([P, S], U8, name="picked_scales")
+        x_plane = sb.tile([P, S], U8, name="x_plane", align_bytes=64)
+        x_plane_tiles = x_plane[:].rearrange("p (g d v) -> p g d v", g=GROUPS, d=D)
         nc.vector.tensor_copy(picked_scales[:], table_scales[:].indirect(offsets[:]))
         quantise_weights(0)
-        nc.vector.tensor_copy(
-            dealt_scales[:].rearrange("p (g d v) -> p g d v", g=GROUPS, d=D),
-            picked_scales[:].rearrange("p (g v d) -> p g d v", g=GROUPS, d=D),
-        )
-        for r in range(4):
-            nc.scalar.dma_start(x_plane[r:P:32, :].bitcast(I32), dealt_scales[8 * r : P : 32, :].bitcast(I32))
+        nc.vector.tensor_copy(x_plane_tiles, picked_scales[:].rearrange("p (g v d) -> p g d v", g=GROUPS, d=D))
+        for r in range(1, 4):
+            nc.scalar.dma_start(x_plane[r:P:32, :].bitcast(I32), x_plane[ROW_STEP * r : P : 32, :].bitcast(I32))
 
-        cols = P * D // 16
+        x_codes = [sb.tile([P, D, P], U32, name=f"x_codes{g}", align_bytes=64) for g in range(GROUPS)]
         for g in range(GROUPS):
             nc.vector.tensor_copy(
                 x_codes[g][:].rearrange("p d v -> p v d"),
-                table_words[:].bitcast(U32).indirect(offsets[:, g * cols : (g + 1) * cols]),
+                table_words[:].bitcast(U32).indirect(offsets[:, g * LIST_COLS : (g + 1) * LIST_COLS]),
             )
-        round_weights(1)
+        nc.vector.tensor_copy(interleaved[1], by_row[1])
         quantise_weights(1)
 
         small = sb.tile([P, 3, GROUPS * D], F32, name="small", tag="w_raw1")
@@ -100,11 +92,11 @@ def tile_picked_ypkpd_eff_p_kernel(
         with nc.allow_non_contiguous_dma(reason="one value a partition"):
             nc.sync.dma_start(ec_t[:, 0:M_BLOCKS], ec50.rearrange("(b p) o -> p (b o)", p=P))
 
-        banks = [(c, g, h) for c in range(2) for g in range(GROUPS) for h in range(D // 2)]
-        NB = len(banks)
+        banks = [(c, g, h) for c in range(RATES) for g in range(GROUPS) for h in range(D // 2)]
+        pairs = len(banks) // RATES
         y = {}
-        ey = sb.tile([P, NB, 2, N], F32, name="ey")
-        u = sb.tile([P, NB, 2, N], F32, name="u")
+        ey = sb.tile([P, len(banks), 2, N], F32, name="ey")
+        u = sb.tile([P, len(banks), 2, N], F32, name="u")
         for b, (c, g, h) in enumerate(banks):
             y[b] = ps.tile([P, 2, N], F32, name=f"y{b}", tag=f"bank{b}")
             for e in range(2):
@@ -112,14 +104,14 @@ def tile_picked_ypkpd_eff_p_kernel(
                 nc.tensor.matmul_mx(
                     out=y[b][:, e, :],
                     lhsT=x_codes[g][:, d, :].bitcast(FP8X4),
-                    lhsT_scale=x_sc[:, g, d, :],
+                    lhsT_scale=x_plane_tiles[:, g, d, :],
                     rhs=w_codes[c][:].bitcast(FP8X4),
                     rhs_scale=w_scales[c][:],
                     start=True,
                     stop=True,
                 )
             nc.scalar.activation(ey[:, b], y[b][:], ACT.Exp)
-            nc.vector.tensor_scalar(u[:, b], ey[:, b], LN_CAP, 1.0, ALU.min, ALU.add)
+            nc.vector.tensor_scalar(u[:, b], ey[:, b], EXP_CAP, 1.0, ALU.min, ALU.add)
 
         neg_ago = sb.tile([P, GROUPS, D], F32, name="neg_ago")
         slow_scale = sb.tile([P, GROUPS, D], F32, name="slow_scale")
@@ -130,15 +122,15 @@ def tile_picked_ypkpd_eff_p_kernel(
         nc.vector.tensor_scalar(fast_bias[:], ago_t, -0.4, math.log(0.7 / 0.3), ALU.mult, ALU.add)
         nc.vector.tensor_scalar(weight[:], amt_t, 0.3, 0.0, ALU.mult, ALU.add)
 
-        lnu = sb.tile([P, 2, NB // 2, 2 * N], F32, name="lnu")
-        sp = sb.tile([P, NB, 2, N], F32, name="sp")
-        u_pairs = u[:].rearrange("p (c b) e m -> p c b (e m)", c=2)
-        order = []
-        for pair in range(NB // 2):
+        lnu = sb.tile([P, RATES, pairs, 2 * N], F32, name="lnu")
+        sp = sb.tile([P, len(banks), 2, N], F32, name="sp")
+        u_pairs = u[:].rearrange("p (c b) e m -> p c b (e m)", c=RATES)
+        freed = []
+        for pair in range(pairs):
             nc.scalar.activation(lnu[:, :, pair, :], u_pairs[:, :, pair, :], ACT.Ln)
-            for c in range(2):
-                b = c * (NB // 2) + pair
-                order.append(b)
+            for c in range(RATES):
+                b = c * pairs + pair
+                freed.append(b)
                 nc.vector.tensor_tensor(
                     sp[:, b].rearrange("p e m -> p (e m)"), y[b][:].rearrange("p e m -> p (e m)"), lnu[:, c, pair, :], ALU.max
                 )
@@ -150,22 +142,29 @@ def tile_picked_ypkpd_eff_p_kernel(
         def accumulate(q):
             mb, g = quarters[q]
             m_cols = slice(mb * P, (mb + 1) * P)
-            conc[q] = ps.tile([P, P], F32, name=f"conc{q}", tag=f"bank{order[q]}")
+            conc[q] = ps.tile([P, P], F32, name=f"conc{q}", tag=f"bank{freed[q]}")
             for d in range(D):
-                decay = sb.tile([P, 2, P], F32, name=f"decay{q}_{d}")
-                dose = sb.tile([P, 2, P], F32, name=f"dose{q}_{d}")
+                decay = sb.tile([P, RATES, P], F32, name=f"decay{q}_{d}")
+                dose = sb.tile([P, RATES, P], F32, name=f"dose{q}_{d}")
                 fast = banks.index((0, g, d // 2))
                 slow = banks.index((1, g, d // 2))
                 nc.scalar.activation(
-                    decay[:, 0, :], sp[:, fast, d % 2, m_cols], ACT.Exp,
-                    bias=fast_bias[:, g, d : d + 1], scale=neg_ago[:, g, d : d + 1],
+                    decay[:, 0, :],
+                    sp[:, fast, d % 2, m_cols],
+                    ACT.Exp,
+                    bias=fast_bias[:, g, d : d + 1],
+                    scale=neg_ago[:, g, d : d + 1],
                 )
                 nc.scalar.activation(decay[:, 1, :], sp[:, slow, d % 2, m_cols], ACT.Exp, scale=slow_scale[:, g, d : d + 1])
                 nc.vector.tensor_scalar(dose[:], decay[:], weight[:, g, d : d + 1], None, ALU.mult)
-                for c in range(2):
+                for c in range(RATES):
                     nc.tensor.matmul(
-                        conc[q][:], dose[:, c, :], ident[:], is_transpose=True,
-                        start=(d == 0 and c == 0), stop=(d == D - 1 and c == 1),
+                        conc[q][:],
+                        dose[:, c, :],
+                        ident[:],
+                        is_transpose=True,
+                        start=(d == 0 and c == 0),
+                        stop=(d == D - 1 and c == RATES - 1),
                     )
             den[q] = sb.tile([P, P], F32, name=f"den{q}")
             nc.scalar.activation(den[q][:], conc[q][:], ACT.Identity, bias=ec_t[:, mb : mb + 1])

import math
from contextlib import ExitStack

import concourse.mybir as mybir
from concourse.masks import make_identity

K, T, S, D, N = 512, 4096, 1024, 4, 256
P = 128
PACK = 4
GROUPS = S // (P * D)
M_BLOCKS = N // P
RATES = 2
LIST_COLS = P * D // 16
ROW_STEP = 8
RUN = 4
FLOPS = 2 * RATES * K * S * N

EXP_CAP = 2.0**60

F32 = mybir.dt.float32
BF16 = mybir.dt.bfloat16
I32 = mybir.dt.int32
U32 = mybir.dt.uint32
U16 = mybir.dt.uint16
U8 = mybir.dt.uint8
FP8X4 = mybir.dt.float8_e4m3fn_x4
ALU = mybir.AluOpType
ACT = mybir.ActivationFunctionType


def tile_picked_ypkpd_eff_p_kernel(
    tc, x_words, x_scales, w1, w2, ago, amt, ec50, offs, out
):
    nc = tc.nc
    with ExitStack() as ctx:
        sb = ctx.enter_context(tc.tile_pool(name="sb", bufs=1))
        ps = ctx.enter_context(tc.psum_pool(name="ps", bufs=1))

        offsets = sb.tile([P, S // 16], U16, name="offsets")
        nc.sync.dma_start(offsets[:], offs)

        table_scales = sb.tile([P, T], U8, name="table_scales")
        nc.vector.memset(table_scales[:].bitcast(I32), 0)

        w_raw = [sb.tile([P, PACK, N], F32, name=f"w_raw{c}", tag=f"w_raw{c}") for c in range(RATES)]
        table_words = sb.tile([P, T], I32, name="table_words")
        nc.sync.dma_start(w_raw[0][:], w1.rearrange("(p t) m -> p t m", t=PACK))
        nc.sync.dma_start(table_scales[0:P:ROW_STEP, :].bitcast(I32), x_scales[0].bitcast(I32))
        nc.sync.dma_start(table_words[:], x_words[0].rearrange("p n t -> p (n t)").bitcast(I32))
        nc.sync.dma_start(w_raw[1][:], w2.rearrange("(p t) m -> p t m", t=PACK))

        ident = sb.tile([P, P], F32, name="ident")
        make_identity(nc, ident[:])

        w_codes = [sb.tile([P, N], U32, name=f"w_codes{c}", align_bytes=64) for c in range(RATES)]
        w_scales = [sb.tile([P, N], U8, name=f"w_scales{c}", align_bytes=64) for c in range(RATES)]
        w_bf = [sb.tile([P, N, PACK], BF16, name=f"w_bf{c}", align_bytes=64) for c in range(RATES)]
        interleaved = [w_bf[c][:].rearrange("p (a i) t -> p a t i", i=RUN) for c in range(RATES)]
        by_row = [w_raw[c][:].rearrange("p t (a i) -> p a t i", i=RUN) for c in range(RATES)]

        def quantise_weights(c):
            nc.vector.quantize_mx(
                out=w_codes[c][:].bitcast(FP8X4), scales=w_scales[c][:], in_=w_bf[c][:].rearrange("p m t -> p (m t)")
            )

        nc.scalar.activation(interleaved[0], by_row[0], ACT.Copy)

        picked_scales = sb.tile([P, S], U8, name="picked_scales")
        x_plane = sb.tile([P, S], U8, name="x_plane", align_bytes=64)
        x_plane_tiles = x_plane[:].rearrange("p (g d v) -> p g d v", g=GROUPS, d=D)
        nc.vector.tensor_copy(picked_scales[:], table_scales[:].indirect(offsets[:]))
        quantise_weights(0)
        nc.vector.tensor_copy(x_plane_tiles, picked_scales[:].rearrange("p (g v d) -> p g d v", g=GROUPS, d=D))
        for r in range(1, 4):
            nc.scalar.dma_start(x_plane[r:P:32, :].bitcast(I32), x_plane[ROW_STEP * r : P : 32, :].bitcast(I32))

        x_codes = [sb.tile([P, D, P], U32, name=f"x_codes{g}", align_bytes=64) for g in range(GROUPS)]
        for g in range(GROUPS):
            nc.vector.tensor_copy(
                x_codes[g][:].rearrange("p d v -> p v d"),
                table_words[:].bitcast(U32).indirect(offsets[:, g * LIST_COLS : (g + 1) * LIST_COLS]),
            )
        nc.vector.tensor_copy(interleaved[1], by_row[1])
        quantise_weights(1)

        small = sb.tile([P, 3, GROUPS * D], F32, name="small", tag="w_raw1")
        ago_t = small[:, 0, :].rearrange("p (g d) -> p g d", d=D)
        amt_t = small[:, 1, :].rearrange("p (g d) -> p g d", d=D)
        ec_t = small[:, 2, :]
        nc.sync.dma_start(ago_t, ago[0].rearrange("(g p d) -> p g d", g=GROUPS, d=D))
        nc.sync.dma_start(amt_t, amt[0].rearrange("(g p d) -> p g d", g=GROUPS, d=D))
        with nc.allow_non_contiguous_dma(reason="one value a partition"):
            nc.sync.dma_start(ec_t[:, 0:M_BLOCKS], ec50.rearrange("(b p) o -> p (b o)", p=P))

        banks = [(c, g, h) for c in range(RATES) for g in range(GROUPS) for h in range(D // 2)]
        pairs = len(banks) // RATES
        y = {}
        ey = sb.tile([P, len(banks), 2, N], F32, name="ey")
        u = sb.tile([P, len(banks), 2, N], F32, name="u")
        for b, (c, g, h) in enumerate(banks):
            y[b] = ps.tile([P, 2, N], F32, name=f"y{b}", tag=f"bank{b}")
            for e in range(2):
                d = 2 * h + e
                nc.tensor.matmul_mx(
                    out=y[b][:, e, :],
                    lhsT=x_codes[g][:, d, :].bitcast(FP8X4),
                    lhsT_scale=x_plane_tiles[:, g, d, :],
                    rhs=w_codes[c][:].bitcast(FP8X4),
                    rhs_scale=w_scales[c][:],
                    start=True,
                    stop=True,
                )
            nc.scalar.activation(ey[:, b], y[b][:], ACT.Exp)
            nc.vector.tensor_scalar(u[:, b], ey[:, b], EXP_CAP, 1.0, ALU.min, ALU.add)

        neg_ago = sb.tile([P, GROUPS, D], F32, name="neg_ago")
        slow_scale = sb.tile([P, GROUPS, D], F32, name="slow_scale")
        fast_bias = sb.tile([P, GROUPS, D], F32, name="fast_bias")
        weight = sb.tile([P, GROUPS, D], F32, name="weight")
        nc.vector.tensor_scalar(neg_ago[:], ago_t, -1.0, 0.0, ALU.mult, ALU.add)
        nc.vector.tensor_scalar(slow_scale[:], ago_t, -0.4, 0.0, ALU.mult, ALU.add)
        nc.vector.tensor_scalar(fast_bias[:], ago_t, -0.4, math.log(0.7 / 0.3), ALU.mult, ALU.add)
        nc.vector.tensor_scalar(weight[:], amt_t, 0.3, 0.0, ALU.mult, ALU.add)

        lnu = sb.tile([P, RATES, pairs, 2 * N], F32, name="lnu")
        sp = sb.tile([P, len(banks), 2, N], F32, name="sp")
        u_pairs = u[:].rearrange("p (c b) e m -> p c b (e m)", c=RATES)
        freed = []
        for pair in range(pairs):
            nc.scalar.activation(lnu[:, :, pair, :], u_pairs[:, :, pair, :], ACT.Ln)
            for c in range(RATES):
                b = c * pairs + pair
                freed.append(b)
                nc.vector.tensor_tensor(
                    sp[:, b].rearrange("p e m -> p (e m)"), y[b][:].rearrange("p e m -> p (e m)"), lnu[:, c, pair, :], ALU.max
                )

        quarters = [(mb, g) for mb in range(M_BLOCKS) for g in range(GROUPS)]
        conc = {}
        den = {}

        def accumulate(q):
            mb, g = quarters[q]
            m_cols = slice(mb * P, (mb + 1) * P)
            conc[q] = ps.tile([P, P], F32, name=f"conc{q}", tag=f"bank{freed[q]}")
            for d in range(D):
                decay = sb.tile([P, RATES, P], F32, name=f"decay{q}_{d}")
                dose = sb.tile([P, RATES, P], F32, name=f"dose{q}_{d}")
                fast = banks.index((0, g, d // 2))
                slow = banks.index((1, g, d // 2))
                nc.scalar.activation(
                    decay[:, 0, :],
                    sp[:, fast, d % 2, m_cols],
                    ACT.Exp,
                    bias=fast_bias[:, g, d : d + 1],
                    scale=neg_ago[:, g, d : d + 1],
                )
                nc.scalar.activation(decay[:, 1, :], sp[:, slow, d % 2, m_cols], ACT.Exp, scale=slow_scale[:, g, d : d + 1])
                nc.vector.tensor_scalar(dose[:], decay[:], weight[:, g, d : d + 1], None, ALU.mult)
                for c in range(RATES):
                    nc.tensor.matmul(
                        conc[q][:],
                        dose[:, c, :],
                        ident[:],
                        is_transpose=True,
                        start=(d == 0 and c == 0),
                        stop=(d == D - 1 and c == RATES - 1),
                    )
            den[q] = sb.tile([P, P], F32, name=f"den{q}")
            nc.scalar.activation(den[q][:], conc[q][:], ACT.Identity, bias=ec_t[:, mb : mb + 1])

        def saturate(q):
            mb, g = quarters[q]
            inv = sb.tile([P, P], F32, name=f"inv{q}")
            res = sb.tile([P, P], F32, name=f"res{q}")
            halves = [slice(0, P // 2), slice(P // 2, P)]
            for s in halves:
                nc.vector.reciprocal(inv[:, s], den[q][:, s])
            for s in halves:
                nc.vector.tensor_tensor(res[:, s], conc[q][:, s], inv[:, s], ALU.mult)
            nc.sync.dma_start(out[mb * P : (mb + 1) * P, g * P : (g + 1) * P], res[:])

        for q in range(len(quarters)):
            accumulate(q)
            if q > 0:
                saturate(q - 1)
        saturate(len(quarters) - 1)
